import numpy as np, ml_dtypes
CORES = [10,34,74,98]
N = 4
BF = ml_dtypes.bfloat16
W, C, L, H, RO = 4096, 64, 256, 9, 6
ROW = np.arange(16)[:, None]
def parts(rng):
    z = (rng.integers(20, 257, (N, 8, 1, W)) * rng.random((N, 8, 16, W))).astype(np.int64)
    a = 1 + (rng.integers(10, 255, (N, 8, 1, L)) * rng.random((N, 8, 16, L))).astype(np.int64)
    w = rng.integers(0, 16, (N, 8, 16, 1)); e = rng.integers(0, W - 1, (N, 8, 16, L))
    often = np.take_along_axis(rng.integers(0, W - 1, (N, 8, 24)), rng.integers(0, 24, (N, 8, 16 * L)), 2).reshape(e.shape)
    e = np.where(rng.random(e.shape) < 0.1, often, e)
    n = rng.integers(2, 13, (N, 8, 1, L)); u = rng.random(n.shape)
    n = np.where(u < 0.04, 0, np.where(u < 0.07, 1, np.where(u < 0.11, 16, n)))
    return np.where(ROW < n, e, W - 1), a, z, w
def poor(rng, n):
    return np.where(np.argsort(rng.random((16, n)), axis=0) < 17 - H, 0, rng.integers(0, 256, (16, n)))
def pack(e, a, z, w):
    z[..., W - 1] = 0
    return {"bills": np.ascontiguousarray(e.reshape(N, 128, L)).astype(np.int32), "due": np.ascontiguousarray(a.reshape(N, 128, L)).astype(np.float32).astype(BF),
            "z0": np.ascontiguousarray(z.reshape(N, 128, W)).astype(np.float32).astype(BF), "wt": np.ascontiguousarray(w.reshape(N, 128, 1)).astype(np.float32).astype(BF)}
def setup_inputs(rng):
    return pack(*parts(rng))
def setup_inputs_room(rng):
    e, a, z, w = parts(rng); a = rng.integers(1, 41, a.shape); w[:, :, 0] = 1
    for q in range(N):
        for g in range(8):
            o = rng.permutation(W - 1); pay, b = o[:L], o[L:]
            z[q, g][:, b] = poor(rng, len(b)); z[q, g][:, pay] = rng.integers(64, 256, (16, L))
            n = np.full(N, C); d1, d2, d3 = (q + 1) % N, (q + 2) % N, (q + 3) % N
            if g % 4 == 0: n[d2] += 1; n[d3] -= 1
            if g % 4 == 1: n[:] = 0; n[d1] = L
            if g % 4 == 2: n[d1] -= 1; n[q] += 1
            if g % 4 == 3: n[d1] = 0; n[d2] += C
            to = rng.permutation(np.repeat(np.arange(N), n)); k = rng.integers(1, 15, L); top = k + rng.integers(0, 16 - k)
            e[q, g] = np.where(ROW < k, rng.integers(0, W - 1, (16, L)), np.where(ROW == k, pay, np.where(ROW <= top, b[rng.integers(0, len(b), (16, L))], W - 1)))
            s = np.sum(w[q, g] * (z[q, g][:, pay] - a[q, g]), axis=0)
            z[q, g, 0, pay] -= (s - to) % N
    return pack(e, a, z, w)
def setup_inputs_ties(rng):
    e, a, z, w = parts(rng); m = min(8, (W - 1) // L)
    for q in range(N):
        for g in range(8):
            o = rng.permutation(W - 1)[:L * m].reshape(m, L); x = a[q, g][:, None, :]
            n = rng.choice(np.array([0, H - 1, H - 1, H, H, H + 1]), (m, L)); good = np.argsort(rng.random((16, m, L)), axis=0) < n
            u = rng.random((16, m, L)); more = np.where(u < 0.5, 0, np.where(u < 0.65, 1, rng.integers(0, 256, u.shape)))
            if q == 0 and g == 0: more = more * 0
            v = np.where(good, np.minimum(x + more, 255), np.where(rng.random(u.shape) < 0.7, x - 1, 0))
            z[q, g][:, o.reshape(-1)] = v.reshape(16, -1)
            r = ROW - rng.integers(0, 17 - m, L)
            e[q, g] = np.where(r < 0, rng.integers(0, W - 1, (16, L)), np.where(r < m, np.take_along_axis(o, np.clip(r, 0, m - 1), 0), W - 1))
    return pack(e, a, z, w)
def setup_inputs_alike(rng):
    e, a, z, w = parts(rng); a = rng.integers(1, 21, a.shape)
    for q in range(N):
        for g in range(8):
            few = rng.permutation(W - 1)[:(1, 2, 3, 40)[g % 4]]
            if g % 4 == 1: few = np.array([0, W - 2])
            z[q, g][:, few] = rng.integers(160, 256, (16, len(few)))
            e[q, g] = np.where(e[q, g] == W - 1, W - 1, few[rng.integers(0, len(few), (16, L))])
    return pack(e, a, z, w)
def setup_inputs_ends(rng):
    e, a, z, w = parts(rng); a = rng.integers(1, 41, a.shape)
    w[:, 2] = 0; w[:, 3] = 15; w[:, 4] = 0; w[:, 4, :2] = 15; w[:, 4, 2] = 1
    xy = (W - 1) // 15 - 13; left = np.array([xy // 2, xy - xy // 2, W - 1 - 15 * xy])[:, None]; t = L // 4
    for q in range(N):
        for g in range(8):
            o = rng.permutation(W - 1); h, b = o[:W // 2], o[W // 2:]
            z[q, g][:, b] = poor(rng, len(b)); z[q, g][:, h] = rng.integers(128, 256, (16, len(h)))
            ri = h[rng.integers(8, len(h), (16, L))]; po = b[rng.integers(0, len(b), (16, L))]; no = np.full((16, L), W - 1)
            if g == 5:
                z[q, g][:, W - 2] = 200; z[q, g][:, 0] = 150
                u = rng.random((16, L)); ri = np.where(u < 0.1, W - 2, np.where(u < 0.2, 0, ri))
            kind = rng.integers(0, 9, L)[None, :]; some = rng.random((16, L)) < 0.3; one = rng.integers(1, 15, L)
            e[q, g] = np.choose(kind, [no, np.where(ROW == 0, ri, no), ri, np.where(ROW < 15, ri, po), np.where(ROW == 0, ri, po), np.where((ROW % 2 == 0) & (ROW < 14), ri, no),
                                       np.where((ROW > 0) & some, ri, no), np.where(ROW == one, ri, no), np.where((ROW == 15) | (ROW % 4 == 1), ri, no)])
            if g == 0:
                z[q, g][:, h[0]] = 255
                for j in range(2):
                    at = L - 8 + 4 * j; k = int(rng.integers(1, 15))
                    e[q, g][:, at:at + 4] = np.where(ROW < k, ri[:, :1], np.where(ROW == k, h[j], W - 1))
                    a[q, g][:, at:at + 4] = np.full((16, 1), 255) if j == 0 else rng.integers(1, 41, (16, 1))
            if g == 3 or g == 4:
                if g == 3: a[q, g][:, :t] = rng.integers(1, 21, (16, t)); z[q, g][:, h[:t]] = 255
                if g == 4: z[q, g][:3, h[:t]] = a[q, g][:3, :t] + left
                k = rng.integers(1, 15, t)
                e[q, g][:, :t] = np.where(ROW < k, h[rng.integers(t, len(h), (16, t))], np.where(ROW == k, h[:t], W - 1))
    e[:, rng.integers(6, 8)] = W - 1; e[rng.integers(0, N), 1] = W - 1
    return pack(e, a, z, w)
def setup_inputs_spread(rng):
    e, a, z, w = parts(rng)
    z = (np.exp2(8 * rng.random((N, 8, 1, W))) * rng.random(z.shape)).astype(np.int64)
    a = 1 + (np.exp2(7.9 * rng.random((N, 8, 1, L))) * rng.random(a.shape)).astype(np.int64)
    w = (16 * rng.random(w.shape) ** 3).astype(np.int64)
    e = np.where(e == W - 1, W - 1, np.minimum(((W - 1) * rng.random(e.shape) ** 2).astype(np.int64), W - 2))
    return pack(e, a, z, w)
def check_inputs(d):
    bad = []
    for k, lo, hi in (("bills", 0, W - 1), ("due", 1, 255), ("z0", 0, 255), ("wt", 0, 15)):
        v = np.asarray(d[k]).astype(np.float32)
        if not np.all((v >= lo) & (v <= hi) & (v == np.floor(v))): bad.append("range of " + k)
    if np.any(np.asarray(d["z0"]).astype(np.float32)[..., W - 1] != 0): bad.append("last column of z0")
    return bad
def reference(bills, due, z0, wt):
    e = bills.astype(np.int64).reshape(N, 8, 16, L); a = due.astype(np.float32).astype(np.int64).reshape(N, 8, 16, L)
    z = z0.astype(np.float32).astype(np.int64).reshape(N, 8, 16, W); w = wt.astype(np.float32).astype(np.int64).reshape(N, 8, 16, 1)
    lower = np.tri(L, k=-1).astype(bool)
    for rnd in range(RO):
        after = []; where_to = []
        for q in range(N):
            v = np.take_along_axis(z[q], e[q].reshape(8, 1, 16 * L), 2).reshape(8, 16, 16, L)
            covers = np.add.reduce((v >= a[q][:, :, None, :]).astype(np.int64), axis=1)
            k = np.max(np.where(covers >= H, ROW, -1), axis=1)
            has = k >= 0; x = np.take_along_axis(e[q], np.maximum(k, 0)[:, None, :], 1)[:, 0]
            x = np.where(has, x, W - 1)
            wait = has & np.any((x[:, :, None] == x[:, None, :]) & lower, axis=2); pays = has & ~wait
            new = np.maximum(np.take_along_axis(z[q], x[:, None, :], 2) - a[q], 0)
            for g in range(8):
                zg = z[q, g]; m = pays[g]; zg[:, x[g][m]] = new[g][:, m]
            c = np.add.reduce(w[q] * new, axis=1) & (W - 1)
            go = pays & (k > 0) & (k < 15); kk = k[:, None, :]
            longer = np.where(ROW <= kk, e[q], np.where(ROW == kk + 1, c[:, None, :], W - 1))
            after.append(np.where(go[:, None, :], longer, e[q]))
            where_to.append(np.where(wait, q, np.where(go, c & (N - 1), -1)))
        e2 = np.full((N, 8, 16, L), W - 1, np.int64); a2 = np.ones((N, 8, 16, L), np.int64)
        for q in range(N):
            for g in range(8):
                for d in range(N):
                    ln = np.flatnonzero(where_to[q][g] == d)[:C]; at = C * q; h = (g + (d != q)) % 8
                    e2[d, h][:, at:at + len(ln)] = after[q][g][:, ln]
                    a2[d, h][:, at:at + len(ln)] = a[q, g][:, ln]
        e, a = e2, a2
    return {"yz": z.reshape(N, 128, W).astype(np.float32).astype(BF), "ye": e.reshape(N, 128, L).astype(np.float32), "ya": a.reshape(N, 128, L).astype(np.float32).astype(BF)}

from concourse.mybir import AluOpType, AxisListType, ActivationFunctionType

OP = AluOpType
AF = ActivationFunctionType
N, W, C, L, RO = 4, 4096, 64, 256, 6
BIG = 8192.0
EMPTY = 2048.0 + 1.0 / 256
SW = 5 * L
AHEAD = 2
NV = ((32, 8, 8, 10), (28, 28, 8, 8))
U1, U2, U3 = 1, 5, 15

SCRATCH = {}
for _n, _c, _d in (
    ("z", W + L, "bfloat16"), ("v", W, "bfloat16"), ("cmp", W, "bfloat16"),
    ("sw", RO * SW, "float32"), ("land", RO * L, "float32"),
    ("bi", L, "int32"), ("ad", L, "bfloat16"), ("a", L, "bfloat16"), ("wb", 8, "bfloat16"), ("e16", L, "uint16"), ("ef", L, "float16"),
    ("yef", L, "float32"), ("yaf", L, "bfloat16"),
    ("sv", L, "bfloat16"), ("ks", L, "bfloat16"), ("y", L, "float16"), ("xr", L, "float16"), ("xs", L, "float32"),
    ("xt16", 16, "uint16"), ("zx", L, "bfloat16"), ("nw", L, "bfloat16"), ("qb", L, "bfloat16"),
    ("r1", L, "float32"), ("r2", L, "float32"), ("b1", L, "float32"), ("b2", L, "float32"), ("ri", L, "int32"), ("nd", L, "bfloat16"),
    ("m", L, "bfloat16"), ("s", L, "float16"), ("val", L, "float16"),
    ("offr", 16, "uint16"), ("offz", 16, "uint16"), ("zt", 16, "float32"),
    ("g0", 128, "bfloat16"), ("pi", 2, "int32"), ("cm", L, "bfloat16"),
    ("u16r", 16, "float32"), ("col", 16, "float32"), ("eq", 16, "float32"), ("pe", 16, "float32"), ("tl", 16, "float32"),
    ("emp", C, "float32"), ("iwb", L, "bfloat16"), ("gm", L, "bfloat16"), ("iw12", L, "bfloat16"), ("iwn", L, "float16"),
    ("iw16", L, "float16"), ("iw32", L, "float32"), ("bo16", 128, "float16"), ("i256", 128, "bfloat16"), ("n256", 128, "bfloat16"),
    ("st", 128, "bfloat16"), ("tk", 128, "bfloat16"), ("tw0", 128, "bfloat16"), ("tw", 128, "bfloat16"),
    ("zc", 128, "bfloat16"), ("zk", 128, "bfloat16"), ("zs", 128, "bfloat16"), ("zo", 128, "bfloat16"), ("zd", 128, "bfloat16"),
    ("yc", 128, "bfloat16"), ("yw", 128, "bfloat16"), ("yk", 128, "bfloat16"), ("cw", 128, "bfloat16"), ("cwn", 128, "bfloat16"),
    ("uk", 128, "bfloat16"), ("up", 128, "bfloat16"),
    ("selb", 144, "bfloat16"), ("selr", 144, "float16"), ("selp", 144, "bfloat16"),
    ("ones", L, "bfloat16"), ("half", 3 * L, "bfloat16"), ("neg", L, "float16"), ("h0", L, "bfloat16"), ("h1", L, "bfloat16"),
    ("thr", L, "bfloat16"), ("dg", L, "bfloat16"), ("pen", L, "bfloat16"), ("rst", L, "bfloat16"),
    ("cr", 16, "float16"), ("dum", 16, "float32"),
):
    SCRATCH[_n] = ("sbuf", [128, _c], _d)
SCRATCH["e3"] = ("sbuf", [128, 16, 272], "bfloat16")
PSUM = ("pa0", "pa1", "pc", "ps1", "ps2", "pw", "px", "pz")
for _n in PSUM:
    SCRATCH[_n] = ("psum", [128, 512], "float32")

SEMAPHORES = ["qv", "qs", "qp", "qg", "ldb", "lda", "ldw", "ldz", "stz", "ste", "sta", "sent"] + [
    "arr%d_%d" % (r, j) for r in range(RO) for j in range(N - 1)]
QSEM = {"V": "qv", "S": "qs", "P": "qp", "G": "qg"}


def emit(g, T, ops):
    queue = {"V": g.vector, "S": g.scalar, "P": g.tensor, "G": g, "Y": g.sync}
    seen = {}
    clock = {q: {} for q in queue}
    after = []
    waits = []
    marked = set()
    for i, o in enumerate(ops):
        key = o["sem"] or QSEM.get(o["q"])
        deps = {}
        both = [(x, False) for x in o["r"]] + [(x, True) for x in o["w"]]
        for (name, lo, hi), wr in both:
            for j, jlo, jhi, jwr in seen.get(name, ()):
                p = ops[j]
                if name in PSUM:
                    need = p["q"] != o["q"]
                else:
                    need = jlo < hi and lo < jhi and (wr or jwr)
                if need:
                    k = p["sem"] or QSEM[p["q"]]
                    deps[k] = max(deps.get(k, -1), j)
        ck = clock[o["q"]]
        mine = []
        for k, j in sorted(deps.items(), key=lambda kv: -kv[1]):
            if ck.get(k, -1) >= j:
                continue
            mine.append(j)
            marked.add(j)
            for kk, jj in after[j].items():
                if ck.get(kk, -1) < jj:
                    ck[kk] = jj
        waits.append(mine)
        snap = dict(ck)
        snap[key] = i
        after.append(snap)
        for (name, lo, hi), wr in both:
            seen.setdefault(name, []).append((i, lo, hi, wr))
    total = {}
    value = {}
    for i, o in enumerate(ops):
        q = queue[o["q"]]
        for j in waits[i]:
            q.wait_ge(T.sem[ops[j]["sem"] or QSEM[ops[j]["q"]]], value[j])
        key = o["sem"] or QSEM.get(o["q"])
        ins = o["f"]() if o["f"] else None
        if o["sem"]:
            total[key] = total.get(key, 0) + o["n"]
            if o["kind"] == "dma":
                ins.then_inc(T.sem[key], o["n"])
        elif i in marked:
            total[key] = total.get(key, 0) + 1
            ins.then_inc(T.sem[key], 1)
        value[i] = total.get(key, 0)
    for key in sorted(total):
        g.wait_ge(T.sem[key], total[key])


def rank_program(g, core, T, topo):
    q = T.rank_of(core)
    if q is None:
        return
    ops = []

    def A(name, lo=0, hi=None, step=1):
        t = T[name]
        if hi is None:
            hi = t.shape[1]
        ap = t[:, lo:hi] if step == 1 else t[:, lo:hi:step]
        return (ap, [(name, lo, hi)])

    def IND(win, off):
        return (win[0].indirect(off[0]), win[1], off[1])

    def add(qn, f, outs, ins, sem=None, n=0, kind=None):
        r, w = [], []
        for x in ins:
            if isinstance(x, tuple):
                r += x[1]
                if len(x) > 2:
                    r += x[2]
        for x in outs:
            w += x[1]
            if len(x) > 2:
                r += x[2]
        ops.append({"q": qn, "f": f, "r": r, "w": w, "sem": sem, "n": n, "kind": kind})

    def val(x):
        return x[0] if isinstance(x, tuple) else x

    def cp(o, i):
        add("V", lambda: g.vector.tensor_copy(o[0], i[0]), [o], [i])

    def tt(o, i0, i1, op):
        add("V", lambda: g.vector.tensor_tensor(o[0], i0[0], i1[0], op), [o], [i0, i1])

    def ts(o, i, s1, op0, s2=None, op1=None):
        if op1 is None:
            add("V", lambda: g.vector.tensor_scalar(o[0], i[0], val(s1), None, op0), [o], [i, s1])
        else:
            add("V", lambda: g.vector.tensor_scalar(o[0], i[0], val(s1), val(s2), op0, op1), [o], [i, s1, s2])

    def scan(o, d0, d1, init, op0, op1):
        add("V", lambda: g.vector.tensor_tensor_scan(o[0], d0[0], d1[0], val(init), op0, op1), [o], [d0, d1, init])

    def ms(o, c):
        add("V", lambda: g.vector.memset(o[0], c), [o], [])

    def act(o, i, func, bias=0.0, scale=1.0):
        add("S", lambda: g.scalar.activation(o[0], i[0], func, bias=val(bias), scale=val(scale)), [o], [i, bias, scale])

    def scaled(o, i, c):
        act(o, i, AF.Identity, 0.0, c)

    def mm(o, lt, rh, start, stop):
        add("P", lambda: g.tensor.matmul(o[0], lt[0], rh[0], start, stop), [o], [lt, rh])

    def iota(o, pat, base, chm, flt=False):
        if flt:
            add("G", lambda: g.iota(o[0], pat, base, chm, allow_small_or_imprecise_dtypes=True), [o], [])
        else:
            add("G", lambda: g.iota(o[0], pat, base, chm), [o], [])

    def select(o, i, pat, op, base, chm):
        add("G", lambda: g.affine_select(o[0], i[0], pat, op, 0.0, base, chm), [o], [i])

    def dma(qn, sem, o, i):
        eng = g.sync if qn == "Y" else g.scalar
        add(qn, lambda: eng.dma_start(o[0], i[0]), [o], [i], sem=sem, n=16, kind="dma")

    def hbm(name):
        return (T[name][:], [])

    def col(k):
        return A("col", k, k + 1)

    def eqc(k):
        return A("eq", k, k + 1)

    def same(name):
        return A(name, 0, 128)

    def up(name, extra=0):
        return A(name, 112 - extra, 240 - extra)

    def down(name):
        return A(name, 16, 144)

    def sel(name, r):
        return A(name, 15 - r, 143 - r)

    def extract(out, name, src):
        for r in range(16):
            mm(out, sel(name, r), A(src, r, L, 16), False, r == 15)

    def fills(rnd):
        for j in range(N):
            select(A("sw", rnd * SW + L * j, rnd * SW + L * j + C), A("emp"), [[0, C]], OP.is_ge, 0, 0)

    dma("S", "ldb", A("bi"), hbm("bills"))
    dma("Y", "ldz", A("z", 0, W), hbm("z0"))
    dma("S", "lda", A("ad"), hbm("due"))
    dma("S", "ldw", A("wb", 0, 1), hbm("wt"))

    PM, YB, KB, INI, YD, POW, WC, ZA, LE3 = range(9)
    ms(A("ones"), 1.0)
    iota(A("pi", 0, 1), [[0, 1]], 0, 1)
    select(same("iwb"), same("ones"), [[-1, 128]], OP.is_equal, 0, 1)
    select(A("g0"), same("ones"), [[-16, 8], [0, 16]], OP.is_ge, 0, 1)
    select(same("gm"), A("g0"), [[16, 8], [0, 16]], OP.is_ge, 15, -1)
    iota(A("cm"), [[0, 16], [1, 16]], 0, 0, True)
    select(A("st"), same("gm"), [[-1, 128]], OP.is_gt, 0, 1)
    iota(A("u16r"), [[16, 16]], 0, 0, True)
    ms(A("selb"), 0.0)
    ms(A("selr"), 0.0)
    ms(A("selp"), 0.0)
    ms(A("yk"), 0.0)
    ms(A("half", 0, L), 0.5)
    ms(A("half", L, 3 * L), 0.0)
    ms(A("neg"), -1.0)
    ms(A("emp"), EMPTY)
    ts(A("pi", 1, 2), A("pi", 0, 1), 15, OP.bitwise_and)
    cp(A("iwb", 128, L), same("iwb"))
    cp(col(PM), A("pi", 1, 2))
    fills(0)
    cp(A("iw16"), A("iwb"))
    ts(col(YB), col(PM), 4096.0, OP.mult, -65536.0, OP.add)
    ts(col(KB), col(PM), -1.0, OP.mult, 15.0, OP.add)
    ts(col(INI), col(PM), 256.0, OP.mult, -1024.0, OP.add)
    ts(col(YD), col(PM), -0.25, OP.mult, -(q + 1) / 4.0, OP.add)
    ts(col(LE3), col(PM), 3.5, OP.is_lt)
    ts(A("iwn"), A("iwb"), -1.0, OP.mult)
    cp(A("gm", 128, L), same("gm"))
    cp(A("selb", 15, 143, 16), A("gm", 0, 128, 16))
    cp(A("bo16"), same("gm"))
    scaled(A("i256"), same("iwb"), 256.0)
    scaled(A("n256"), same("iwb"), -256.0)
    scaled(A("iw12"), A("iwb"), 4096.0)
    scaled(A("iw32"), A("iwb"), 1.0)
    scaled(A("zs"), same("iwb"), 1.0)
    scaled(A("zc"), same("iwb"), -2.0)
    scaled(A("yc"), same("iwb"), col(YD))
    scaled(A("zo"), up("gm"), -1.0)
    scaled(A("zs", 3, 128, 16), A("iwb", 3, 128, 16), -1.0)
    scaled(A("zc", 3, 128, 16), A("iwb", 3, 128, 16), 0.0)
    scaled(A("zc", 4, 128, 16), A("iwb", 4, 128, 16), -1.0)
    scaled(A("yc", 3, 128, 16), A("iwb", 3, 128, 16), 0.125 - (q + 4) / 4.0)
    scaled(A("yc", 4, 128, 16), A("iwb", 4, 128, 16), 0.0)
    scaled(A("zo", 3, 128, 16), A("gm", 115, 240, 16), 1.0)
    ts(A("eq"), A("cm", 0, 16), col(PM), OP.is_equal)
    ts(A("h0"), A("cm"), 0.0, OP.is_gt, 0.5, OP.mult)
    ts(A("h1"), A("cm"), 0.0, OP.is_equal, 0.625, OP.mult)
    ts(A("dg"), A("cm"), col(PM), OP.is_equal)
    tt(A("tw0"), same("iwb"), A("st"), OP.subtract)
    cp(col(WC), A("wb", 0, 1))
    tt(A("uk"), up("iw12", 1), up("iw12"), OP.subtract)
    scan(A("thr"), A("h0"), A("h1"), 0.0, OP.mult, OP.add)
    cp(A("e16"), A("bi"))
    ts(A("ef"), A("bi"), -2047.0, OP.add)
    ts(A("a"), A("ad"), 1.0 / 256, OP.mult)
    act(A("pen"), A("dg"), AF.Identity, -32768.0, 65536.0)
    scaled(A("tw"), A("tw0"), 4096.0)
    scaled(A("cw"), up("gm"), col(WC))
    scaled(A("uk", 0, 128, 16), A("iwb", 0, 128, 16), 0.0)
    scaled(A("yw"), A("cw"), 0.25)
    scaled(A("cwn"), A("cw"), -1.0)
    scaled(A("yw", 4, 128, 16), A("iwb", 4, 128, 16), 0.0)
    ts(A("tl"), A("u16r"), col(PM), OP.add)
    ts(A("rst"), A("h0"), 131072.0, OP.mult, 0.5, OP.max)
    tt(col(ZA), eqc(1), eqc(15), OP.subtract)
    tt(A("pe"), A("eq"), A("thr", 0, 16), OP.mult)
    ts(A("selr", 15, 143, 16), A("gm", 0, 128, 16), col(LE3), OP.mult)
    ts(A("selp", 15, 143, 16), A("gm", 16, 144, 16), eqc(4), OP.mult, -65536.0, OP.mult)
    ts(A("zk"), up("gm"), col(ZA), OP.mult)
    add("V", lambda: g.vector.tensor_reduce(T.col[:, POW:POW + 1], T.pe[:], AxisListType.X, OP.add), [col(POW)], [A("pe")])
    ts(A("cr"), A("tl"), 1024.0, OP.add)
    ts(A("dum"), A("tl"), 4097.0 - 65536.0, OP.add)
    ts(A("yk", 3, 128, 16), A("gm", 115, 240, 16), col(ZA), OP.mult, -0.0625, OP.mult)
    ts(A("zk", 4, 128, 16), A("gm", 116, 240, 16), eqc(0), OP.mult)
    tt(A("tk"), same("iwb"), A("st"), OP.add)
    ts(A("up"), same("gm"), eqc(4), OP.mult, BIG, OP.mult)
    ts(A("zk", 3, 128, 16), A("gm", 115, 240, 16), eqc(0), OP.mult)
    ts(A("zd"), A("zo"), col(POW), OP.mult, 0.4, OP.mult)

    def near(o):
        return all(topo.same_plane(topo.chip(T.cores[r]), topo.chip(T.cores[(r + o) % N])) for r in range(N))

    steps = sorted(range(1, N), key=lambda o: not near(o))
    order = [q] + [(q - o) % N for o in steps]
    first = (C * q, C * q + C)
    late = (C * order[N - 1], C * order[N - 1] + C)
    lo1, lo2 = sorted(C * b for b in order[1:3])
    early = [(lo1, lo2 + C)] if lo1 + C == lo2 else [(lo1, lo1 + C), (lo2, lo2 + C)]
    zwin = A("z", 0, W)

    def lanes(i):
        return C * order[i], C * order[i] + C

    def packed(rnd, b):
        if b == q:
            return A("px", C, 2 * C)
        return A("land", rnd * L + C * b, rnd * L + C * b + C)

    def names(rnd, i):
        if rnd < 0:
            return
        pk = packed(rnd, order[i])
        if i > 0:
            add("V", None, [pk], [], sem="arr%d_%d" % (rnd, i - 1), n=len(topo.engines(T.cores[order[i]], core)), kind="arr")
        ts(A("e16", *lanes(i)), pk, 2046.5, OP.add)

    def names16(rnd, i):
        if rnd >= 0:
            ts(A("ef", *lanes(i)), A("e16", *lanes(i)), -2047.0, OP.add)

    def amounts(rnd, i):
        if rnd >= 0:
            tt(A("a", *lanes(i)), packed(rnd, order[i]), A("ef", *lanes(i)), OP.subtract)

    def gather_s(i, rnd):
        lo, hi = C * order[i] + NV[rnd > 0][i], C * order[i] + C
        act(A("v", 16 * lo, 16 * hi), IND(zwin, A("e16", lo, hi)), AF.Copy)

    def gather_v(i, rnd):
        lo, hi = C * order[i], C * order[i] + NV[rnd > 0][i]
        cp(A("v", 16 * lo, 16 * hi), IND(zwin, A("e16", lo, hi)))

    def expand(i, h):
        for j in range(8):
            mm(A("pa%d" % h, j, 512, 8), A("i256"), A("a", *lanes(i)), True, True)

    def compare(i, h):
        o = 1024 * order[i]
        tt(A("cmp", o + 512 * h, o + 512 * h + 512), A("v", o + h, o + 1024, 2), A("pa%d" % h), OP.is_ge)

    def covers(lo, hi):
        if (lo, hi) == late:
            return A("px", L, L + C)
        return A("px", L + C, L + 2 * C) if (lo, hi) == first else A("pc", lo, hi)

    def count(i, h):
        o = 1024 * order[i] + 512 * h
        for j in range(8):
            mm(covers(*lanes(i)), sel("selb", 2 * j + h), A("cmp", o + j, o + 512, 8), h == 0 and j == 0, h == 1 and j == 7)

    def compare_q(i, h, k):
        o = 1024 * order[i]
        tt(A("cmp", o + 512 * h + 256 * k, o + 512 * h + 256 * k + 256), A("v", o + h + 2 * k, o + 1024, 4), A("pa%d" % h, k, 512, 2), OP.is_ge)

    def count_q(i, h, k):
        o = 1024 * order[i] + 512 * h + 256 * k
        for j in range(4):
            mm(covers(*lanes(i)), sel("selb", 4 * j + 2 * k + h), A("cmp", o + j, o + 256, 4), False, k == 1 and j == 3)

    def sums(i):
        lo, hi = lanes(i)
        mm(A("ps1", lo, hi), A("n256"), A("a", lo, hi), False, False)
        mm(A("ps1", L + lo, L + hi), up("iwn"), A("ef", lo, hi), False, False)
        mm(A("ps2", lo, hi), up("iwb"), A("a", lo, hi), False, False)
        mm(A("ps2", L + lo, L + hi), up("iwb"), A("a", lo, hi), False, False)
        mm(A("ps2", L + lo, L + hi), up("iw16"), A("ef", lo, hi), False, False)

    def solvent(parts):
        for lo, hi in parts:
            act(A("sv", lo, hi), covers(lo, hi), AF.Sign, -8.5)

    def top_pe(parts):
        for lo, hi in parts:
            mm(A("pw", lo, hi), same("iw16"), A("ef", lo, hi), True, False)
            mm(A("pw", lo, hi), A("tw"), A("sv", lo, hi), False, True)

    def top_v(parts):
        for lo, hi in parts:
            ts(A("y", lo, hi), A("pw", lo, hi), col(YB), OP.add, -2048.0, OP.max)

    def rowp(lo, hi, k=0):
        if (lo, hi) in (first, late):
            return A("pw", L + C * k, L + C * k + C)
        return A("pa0", L * k + lo, L * k + hi)

    def row_pe(parts):
        for lo, hi in parts:
            mm(rowp(lo, hi, 1), A("bo16"), A("y", lo, hi), True, False)
            mm(rowp(lo, hi, 1), same("iwb"), A("pen", lo, hi), False, True)
            mm(rowp(lo, hi), A("bo16"), A("y", lo, hi), True, True)

    def list_v(parts):
        for lo, hi in parts:
            scan(A("xs", lo, hi), A("rst", lo, hi), rowp(lo, hi, 1), 0.5, OP.min, OP.max)

    def row_v(parts):
        for lo, hi in parts:
            ts(A("xr", lo, hi), rowp(lo, hi), 30720.0, OP.add)

    for rnd in range(RO):
        gather_s(0, rnd)
        names16(rnd - 1, 0)
        mm(A("pz", 0, L), A("zc"), A("ones"), True, False)
        mm(A("pz", 0, L), A("zs"), A("thr"), False, False)
        amounts(rnd - 1, 0)
        gather_v(0, rnd)
        expand(0, 0)
        expand(0, 1)
        mm(A("ps2"), same("iw12"), A("half", 0, 2 * L), True, False)
        mm(A("ps1"), same("iw12"), A("half", L, 3 * L), True, False)
        sums(0)
        at = 2 if rnd > 0 else 3
        for i in range(1, N):
            ahead = AHEAD if i == 1 and rnd > 0 else 0
            for h in range(ahead):
                compare(0, h)
                count(0, h)
            names(rnd - 1, i)
            gather_s(i, rnd)
            if i == at:
                top_pe([first])
            if ahead < 1:
                compare(i - 1, 0)
            names16(rnd - 1, i)
            if i == at:
                top_v([first])
            if ahead < 1:
                count(i - 1, 0)
            if i == at:
                row_pe([first])
            if ahead == 2:
                amounts(rnd - 1, i)
            gather_v(i, rnd)
            if ahead < 2:
                amounts(rnd - 1, i)
                compare(i - 1, 1)
            if i == at:
                list_v([first])
                row_v([first])
            expand(i, 0)
            if i == N - 1:
                sums(i)
            expand(i, 1)
            if ahead < 2:
                count(i - 1, 1)
            if i == at - 1:
                solvent([first])
            if i < N - 1:
                sums(i)
        solvent(early)
        compare(N - 1, 0)
        count(N - 1, 0)
        top_pe(early)
        compare_q(N - 1, 1, 0)
        count_q(N - 1, 1, 0)
        compare_q(N - 1, 1, 1)
        top_v(early)
        count_q(N - 1, 1, 1)
        solvent([late])
        row_pe(early)
        top_pe([late])
        top_v([late])
        list_v(early)
        mm(A("pc", L, 2 * L), A("tk"), A("sv"), True, True)
        row_pe([late])
        row_v(early)
        act(A("ks"), A("pc", L, 2 * L), AF.Sign, col(KB))
        mm(A("pa1", 0, L), A("yc"), A("ones"), True, False)
        list_v([late])
        row_v([late])
        ts(A("xt16"), A("xs", 15, L, 16), -1.0, OP.add, 0.0, OP.max)
        act(A("zx"), IND(zwin, A("xt16")), AF.Copy)
        mm(A("pz", 0, L), A("zk"), A("ks"), False, False)
        mm(A("pa1", 0, L), A("yk"), A("ks"), False, False)
        mm(A("ps1", L, 2 * L), up("iw12"), A("ks"), False, False)

        for u in range(16):
            n = L - 16 * u
            ext = [("e3", 272 * u, 272 * u + n)]
            ts((T.e3[:, u, 0:n], ext), A("xr", 16 * u, L), A("xs", 16 * u + 15, 16 * u + 16), OP.subtract, -2048.0, OP.is_equal)
            if u < 15:
                mm(A("pz", 16 * u + 16, L), A("zo"), (T.e3[:, u, 16:n], ext), False, False)
            if u % 8 == 7:
                mm(A("pz", 16 * u - 112, 16 * u + 16), A("zd"),
                   (T.e3[:, u - 7:u + 1, 0:16], [("e3", 272 * (u - 7), 272 * u + 16)]), False, u == 15)
            if u == U1:
                mm(A("ps1", 0, L), same("iwb"), A("zx"), False, True)
                act(A("nw"), A("ps1", 0, L), AF.Relu)
                act(A("r1"), A("ps1", L, 2 * L), AF.Relu, 2048.0 - BIG / 2)
            if u == U2:
                mm(A("pa1", 0, L), A("yw"), A("nw"), False, True)
            if u == U3:
                mm(A("pc", 0, L), A("cw"), A("nw"), True, True)
                act(A("qb"), A("pc", 0, L), AF.Identity, 143.5 + 1.0 / 8192, 1.0 / 4096)
        cp(A("ri"), A("pa1", 0, L))
        tt(A("nd"), A("ri"), A("pa1", 0, L), OP.not_equal)
        mm(A("pa0", 0, L), A("uk"), A("ks"), True, False)
        mm(A("pa0", 0, L), A("cwn"), A("nw"), False, False)
        mm(A("pa0", 0, L), same("iw12"), A("qb"), False, False)

        tt(A("m"), A("pz", 0, L), A("nd"), OP.is_gt)
        mm(A("px", 16, 32), same("iw16"), A("cr"), True, False)
        mm(A("pa0", 0, L), A("up"), A("m"), False, True)
        mm(A("ps2", L, 2 * L), A("up"), A("m"), False, True)
        act(A("r2"), A("pa0", 0, L), AF.Relu, 4095.0 - 144 * 4096 - 2 * BIG)
        scan(A("s"), A("m"), A("neg"), col(INI), OP.add, OP.add)
        tt(A("val"), A("m"), A("s"), OP.mult)
        extract(A("px", 16, 32), "selr", "val")
        tt(A("b1"), A("ps2", 0, L), A("r1"), OP.subtract)
        tt(A("b2"), A("ps2", L, 2 * L), A("b1"), OP.min)
        cp(A("offr"), A("px", 16, 32))
        tt(IND(A("sw", rnd * SW, rnd * SW + SW), A("offr")), A("b2"), A("r2"), OP.subtract)
        for j, o in enumerate(steps):
            dst = T.cores[(q + o) % N]
            rid, pid, _e = topo.addr(dst)
            src = A("sw", rnd * SW + L * (o - 1), rnd * SW + L * (o - 1) + C)
            out = T.land[:, rnd * L + C * q:rnd * L + C * q + C]

            def send(out=out, src=src, j=j, pid=pid, rid=rid, dst=dst, rnd=rnd):
                return g.remote_dma(out, src[0], T.sem["arr%d_%d" % (rnd, j)], T.sem.sent, pid, rid, topo.mask(core, dst))

            add("G", send, [], [src], sem="sent", n=len(topo.engines(core, dst)), kind="remote")
        if rnd + 1 < RO:
            fills(rnd + 1)

        mm(A("ps1", 0, 16), same("iw32"), A("xs", 15, L, 16), True, False)
        extract(A("ps1", 0, 16), "selp", "m")
        mm(A("px", C, 2 * C), down("iw32"), A("sw", rnd * SW + 3 * L, rnd * SW + 3 * L + C), True, True)
        tt(A("zt"), A("ps1", 0, 16), A("dum"), OP.min)
        ts(A("offz"), A("zt"), 65535.0, OP.add)
        names(rnd, 0)
        cp(IND(A("z"), A("offz")), A("nw"))

    dma("Y", "stz", hbm("yz"), zwin)
    for i in range(N):
        lo, hi = lanes(i)
        if i > 0:
            names(RO - 1, i)
        names16(RO - 1, i)
        cp(A("yef", lo, hi), A("e16", lo, hi))
        amounts(RO - 1, i)
        scaled(A("yaf", lo, hi), A("a", lo, hi), 256.0)
    dma("Y", "ste", hbm("ye"), A("yef"))
    dma("S", "sta", hbm("ya"), A("yaf"))
    emit(g, T, ops)
